import numpy as np
import ml_dtypes


def mxq(x, axis, fmt="e4m3"):
    dtype, down = {"e4m3": (ml_dtypes.float8_e4m3fn, 7), "e5m2": (ml_dtypes.float8_e5m2, 14)}[fmt]
    v = np.moveaxis(np.asarray(x, np.float32).astype(ml_dtypes.bfloat16).astype(np.float64), axis, -1)
    blocks = v.reshape(v.shape[:-1] + (-1, 32))
    amax = np.abs(blocks).max(-1, keepdims=True)
    byte = np.maximum(np.where(amax > 0, np.frexp(amax)[1] - 1 + 127, 0) - down, 1)
    scale = np.exp2(byte - 127.0)
    codes = (blocks / scale).astype(np.float32).astype(dtype).astype(np.float64)
    return np.moveaxis((codes * scale).reshape(v.shape), -1, axis)


WIDE = False


def mx_kscale(k):
    if not WIDE:
        return np.ones(k)
    levels = np.array([10, -10, 5, -5, 0])
    if k % 512:
        return np.exp2(np.random.permutation(np.resize(levels, k // 32))).repeat(32)
    a = np.empty((k // 512, 16))
    for p in range(k // 512):
        a[p, :8] = np.random.permutation(np.resize(levels, 8))
        for g in range(8):
            far = levels[np.abs(levels - a[p, g]) >= 10]
            a[p, g + 8] = far[np.random.randint(len(far))]
    return np.exp2(a.ravel()).repeat(32)


def f64(x):
    return np.asarray(x).astype(np.float64)


def striped(idx):
    return np.tile(np.asarray(idx).reshape(-1, 16).T, (8, 1)).astype(np.uint16)


def unstriped(offs):
    return offs[:16].T.reshape(-1).astype(np.int64)


E2M1 = np.array([0.0, 0.5, 1.0, 1.5, 2.0, 3.0, 4.0, 6.0, -0.0, -0.5, -1.0, -1.5, -2.0, -3.0, -4.0, -6.0])


def pack_weight(w, fmt):
    k, n = w.shape
    w = f64(np.asarray(w, np.float32).astype(ml_dtypes.bfloat16)).reshape(k // 32, 32, n)
    amax = np.abs(w).max(1)
    if fmt == "e4m3":
        byte = np.frexp(amax)[1] - 1 + 127 - 7
    else:
        mant, ex = np.frexp(amax / 6.0)
        byte = np.where(mant > 0.5, ex, ex - 1) + 127
    byte = np.clip(np.where(amax > 0, byte, 1), 1, 254)
    scaled = (w * np.exp2(127.0 - byte)[:, None, :]).reshape(k, n).astype(np.float32)
    by_word = np.ascontiguousarray(scaled.reshape(k // 512, 128, 4, n).transpose(0, 1, 3, 2))
    if fmt == "e4m3":
        words = by_word.astype(ml_dtypes.float8_e4m3fn).view(np.uint8)
    else:
        c = by_word.astype(ml_dtypes.float4_e2m1fn).view(np.uint8) & 0xF
        words = (c[..., 0::2] | (c[..., 1::2] << 4)).reshape(k // 512, 128, 2 * n)
    return np.ascontiguousarray(words), np.ascontiguousarray(byte.astype(np.uint8).reshape(k // 512, 16, n))


def unpack_weight(words, scales, fmt):
    g, _, n = scales.shape
    words = np.ascontiguousarray(words).reshape(g, 128, n, -1)
    if fmt == "e4m3":
        vals = words.view(ml_dtypes.float8_e4m3fn).astype(np.float64)
    else:
        nib = np.empty((g, 128, n, 4), np.uint8)
        nib[..., 0::2] = words & 0xF
        nib[..., 1::2] = words >> 4
        vals = E2M1[nib]
    vals = vals * np.repeat(np.exp2(scales.astype(np.float64) - 127.0), 8, axis=1)[..., None]
    return vals.transpose(0, 1, 3, 2).reshape(g * 512, n)


B, N, T, D, NQ = 1, 1024, 4096, 1024, 128
SEG = 16


def setup_inputs():
    n = np.random.standard_normal
    pages = np.random.permutation(T // 16)[:B * N // 16]
    idx = (pages[:, None] * 16 + np.arange(16)[None, :]).reshape(-1)
    s = mx_kscale(D)[:, None]
    kp = pack_weight(n((D, T)) / s, "e2m1")
    return {
        "qT": (n((B, D, NQ)) * s * (1.00 / np.sqrt(D))).astype(np.float32),
        "k_words": np.ascontiguousarray(kp[0].reshape(1, 2, 128, T, 2).transpose(0, 2, 3, 1, 4)).reshape(1, 128, T, 4),
        "k_scales": kp[1],
        "offs": striped(idx),
    }


def reference(qT, k_words, k_scales, offs):
    idx = unstriped(offs)
    pick = lambda x, which: x[:, which].reshape(x.shape[0], B, -1).transpose(1, 0, 2)
    k = unpack_weight(k_words.reshape(1, 128, T, 2, 2).transpose(0, 3, 1, 2, 4).reshape(2, 128, 2 * T), k_scales, "e2m1")
    kg = pick(k, idx)
    qq = mxq(f64(qT), 1, "e4m3")
    a = qq.transpose(0, 2, 1) @ kg
    e = np.exp(2.0 * a)
    y = (a * e).reshape(B, NQ, N // SEG, SEG).sum(-1) / e.reshape(B, NQ, N // SEG, SEG).sum(-1)
    return y

@@ -1,0 +1,131 @@
+from contextlib import ExitStack
+
+import concourse.mybir as mybir
+
+F32 = mybir.dt.float32
+BF16 = mybir.dt.bfloat16
+I32 = mybir.dt.int32
+U32 = mybir.dt.uint32
+U16 = mybir.dt.uint16
+U8 = mybir.dt.uint8
+FP8X4 = mybir.dt.float8_e4m3fn_x4
+FP4X4 = mybir.dt.float4_e2m1fn_x4
+ALU = mybir.AluOpType
+ACT = mybir.ActivationFunctionType
+AX = mybir.AxisListType
+
+P = 128
+N, T, D, NQ, SEG = 1024, 4096, 1024, 128, 16
+PASSES = 2
+BANK = 512
+BANKS = N // BANK
+PIECE = 256
+FLOPS = 2 * NQ * D * N
+
+
+def tile_attend_page_smooth_kernel(tc, qT, k_words, k_scales, offs, out):
+    nc = tc.nc
+    with ExitStack() as ctx:
+        lists = ctx.enter_context(tc.tile_pool(name="lists", bufs=1))
+        sb = ctx.enter_context(tc.tile_pool(name="sb", bufs=1))
+        psum = ctx.enter_context(tc.psum_pool(name="psum", bufs=1))
+
+        offsets = lists.tile([P, N // 16], U16, name="offsets")
+        nc.sync.dma_start(offsets[:], offs)
+
+        word_pool = sb.tile([P, T], I32, name="word_pool", align_bytes=64)
+        nc.sync.dma_start(word_pool[:], k_words[0].rearrange("p t b -> p (t b)").bitcast(I32))
+
+        q_raw = []
+        for o in range(PASSES):
+            raw = sb.tile([P, 4, NQ], F32, name="q_raw%d" % o)
+            nc.sync.dma_start(raw[:], qT[0, 512 * o : 512 * (o + 1), :].rearrange("(p r) q -> p r q", r=4))
+            q_raw.append(raw)
+
+        scale_pool = sb.tile([P, PASSES, T // 4], I32, name="scale_pool", align_bytes=64)
+        nc.vector.memset(scale_pool[:, 0, :], 0)
+        nc.gpsimd.memset(scale_pool[:, 1, :], 0)
+        nc.scalar.dma_start(scale_pool[32:96:4, :, :], k_scales.rearrange("o f t -> f o t").bitcast(I32))
+
+        k_plane = sb.tile([P, PASSES, N // 4], I32, name="k_plane", align_bytes=64)
+        nc.vector.memset(k_plane[:], 0)
+
+        scale_picked = sb.tile([P, PASSES, N], U8, name="scale_picked", align_bytes=64)
+        for o in range(PASSES):
+            nc.vector.tensor_copy(scale_picked[:, o, :], scale_pool[:, o, :].bitcast(U8).indirect(offsets[:]))
+        for quad in range(4):
+            first = 32 + 16 * quad
+            nc.scalar.dma_start(k_plane[32 * quad : 32 * quad + 4, :, :], scale_picked[first : first + 16 : 4, :, :].bitcast(I32))
+
+        q_codes = sb.tile([P, PASSES, NQ], U32, name="q_codes", align_bytes=64)
+        q_plane = sb.tile([P, PASSES, NQ], U8, name="q_plane", align_bytes=64)
+        q_bf = []
+        for o in range(PASSES):
+            grouped = sb.tile([P, NQ, 4], BF16, name="q_bf%d" % o, align_bytes=64)
+            nc.scalar.copy(grouped[:], q_raw[o][:].rearrange("p r q -> p q r"))
+            q_bf.append(grouped)
+
+        def quantize(o):
+            nc.vector.quantize_mx(q_codes[:, o, :].bitcast(FP8X4), q_plane[:, o, :], q_bf[o][:].rearrange("p q r -> p (q r)"))
+
+        k_codes = []
+        for b in range(BANKS):
+            picked = sb.tile([P, BANK], U32, name="picked%d" % b, align_bytes=64)
+            nc.vector.tensor_copy(picked[:], word_pool[:].bitcast(U32).indirect(offsets[:, b * BANK // 16 : (b + 1) * BANK // 16]))
+            if b == 1:
+                quantize(1)
+            parted = sb.tile([P, PASSES, BANK], U16, name="parted%d" % b, align_bytes=64)
+            nc.vector.tensor_copy(parted[:], picked[:].bitcast(U16).rearrange("p (n o) -> p o n", o=PASSES))
+            if b == 0:
+                quantize(0)
+            k_codes.append(parted)
+
+        scores = []
+        for b in range(BANKS):
+            acc = psum.tile([P, BANK], F32, name="scores%d" % b)
+            for o in range(PASSES):
+                nc.tensor.matmul_mx(
+                    acc[:],
+                    lhsT=q_codes[:, o, :].bitcast(FP8X4),
+                    lhsT_scale=q_plane[:, o, :],
+                    rhs=k_codes[b][:, o, :].bitcast(FP4X4),
+                    rhs_scale=k_plane[:, o, :].bitcast(U8)[:, b * BANK : (b + 1) * BANK],
+                    start=(o == 0),
+                    stop=(o == PASSES - 1),
+                )
+            scores.append(acc)
+
+        runs = N // SEG
+        peak = sb.tile([P, runs], F32, name="peak")
+        below = sb.tile([P, runs, SEG], F32, name="below")
+        weight = sb.tile([P, runs, SEG], F32, name="weight")
+        weighted = sb.tile([P, runs, SEG], F32, name="weighted")
+        den = sb.tile([P, runs], F32, name="den")
+        num = sb.tile([P, runs], F32, name="num")
+        inv = sb.tile([P, runs], F32, name="inv")
+        mean = sb.tile([P, runs], F32, name="mean")
+        res = sb.tile([P, runs], F32, name="res")
+        rb = BANK // SEG
+        rp = PIECE // SEG
+        for b in range(BANKS):
+            a3 = scores[b][:].rearrange("p (j s) -> p j s", s=SEG)
+            halves = range(BANK // PIECE)
+            for h in halves:
+                js = slice(b * rb + h * rp, b * rb + (h + 1) * rp)
+                nc.vector.tensor_reduce(peak[:, js], a3[:, h * rp : (h + 1) * rp, :], AX.X, ALU.max)
+            for h in halves:
+                js = slice(b * rb + h * rp, b * rb + (h + 1) * rp)
+                nc.vector.tensor_tensor(below[:, js, :], a3[:, h * rp : (h + 1) * rp, :], peak[:, js].unsqueeze(2).to_broadcast([P, rp, SEG]), ALU.subtract)
+                nc.scalar.activation(weight[:, js, :], below[:, js, :], ACT.Exp, scale=2.0)
+                nc.gpsimd.tensor_tensor(weighted[:, js, :], below[:, js, :], weight[:, js, :], ALU.mult)
+        for b in range(BANKS):
+            js = slice(b * rb, (b + 1) * rb)
+            j0 = slice(b * rb, b * rb + rp)
+            j1 = slice(b * rb + rp, (b + 1) * rb)
+            nc.vector.tensor_reduce(den[:, js], weight[:, js, :], AX.X, ALU.add)
+            nc.vector.tensor_reduce(num[:, j0], weighted[:, j0, :], AX.X, ALU.add)
+            nc.vector.reciprocal(inv[:, js], den[:, js])
+            nc.vector.tensor_reduce(num[:, j1], weighted[:, j1, :], AX.X, ALU.add)
+        nc.vector.tensor_tensor(mean[:], num[:], inv[:], ALU.mult)
+        nc.vector.tensor_tensor(res[:], mean[:], peak[:], ALU.add)
+        nc.sync.dma_start(out[0], res[:])

@@ -30,69 +30,78 @@ def tile_attend_page_smooth_kernel(tc, qT, k_words, k_scales, offs, out):
         sb = ctx.enter_context(tc.tile_pool(name="sb", bufs=1))
         psum = ctx.enter_context(tc.psum_pool(name="psum", bufs=1))
 
+        scale_pool = sb.tile([P, T // 4], I32, name="scale_pool", tag="staged", align_bytes=64)
+        nc.sync.dma_start(scale_pool[0:32, :], k_scales.rearrange("o f t -> (o f) t").bitcast(I32))
         offsets = lists.tile([P, N // 16], U16, name="offsets")
         nc.sync.dma_start(offsets[:], offs)
+        nc.vector.memset(scale_pool[32:64, :], 0)
+        nc.gpsimd.memset(scale_pool[64:128, :], 0)
 
         word_pool = sb.tile([P, T], I32, name="word_pool", align_bytes=64)
         nc.sync.dma_start(word_pool[:], k_words[0].rearrange("p t b -> p (t b)").bitcast(I32))
 
-        q_raw = []
-        for o in range(PASSES):
-            raw = sb.tile([P, 4, NQ], F32, name="q_raw%d" % o)
-            nc.sync.dma_start(raw[:], qT[0, 512 * o : 512 * (o + 1), :].rearrange("(p r) q -> p r q", r=4))
-            q_raw.append(raw)
-
-        scale_pool = sb.tile([P, PASSES, T // 4], I32, name="scale_pool", align_bytes=64)
-        nc.vector.memset(scale_pool[:, 0, :], 0)
-        nc.gpsimd.memset(scale_pool[:, 1, :], 0)
-        nc.scalar.dma_start(scale_pool[32:96:4, :, :], k_scales.rearrange("o f t -> f o t").bitcast(I32))
 
         k_plane = sb.tile([P, PASSES, N // 4], I32, name="k_plane", align_bytes=64)
         nc.vector.memset(k_plane[:], 0)
 
-        scale_picked = sb.tile([P, PASSES, N], U8, name="scale_picked", align_bytes=64)
+        scale_picked = sb.tile([P, N], U8, name="scale_picked", align_bytes=64)
+        nc.vector.tensor_copy(scale_picked[:], scale_pool[:].bitcast(U8).indirect(offsets[:]))
+        moves = [(o, quad) for o in range(PASSES) for quad in range(4)]
+
+        def move(o, quad):
+            first = 16 * o + 4 * quad
+            nc.sync.dma_start(k_plane[32 * quad : 32 * quad + 4, o, :], scale_picked[first : first + 4, :].bitcast(I32))
+
+        for o, quad in moves[:5]:
+            move(o, quad)
+        q_raw = sb.tile([P, PASSES, 4, NQ], F32, name="q_raw", tag="staged", align_bytes=64)
         for o in range(PASSES):
-            nc.vector.tensor_copy(scale_picked[:, o, :], scale_pool[:, o, :].bitcast(U8).indirect(offsets[:]))
-        for quad in range(4):
-            first = 32 + 16 * quad
-            nc.scalar.dma_start(k_plane[32 * quad : 32 * quad + 4, :, :], scale_picked[first : first + 16 : 4, :, :].bitcast(I32))
+            nc.sync.dma_start(q_raw[:, o], qT[0, 512 * o : 512 * (o + 1), :].rearrange("(p r) q -> p r q", r=4))
+        for o, quad in moves[5:]:
+            move(o, quad)
 
         q_codes = sb.tile([P, PASSES, NQ], U32, name="q_codes", align_bytes=64)
         q_plane = sb.tile([P, PASSES, NQ], U8, name="q_plane", align_bytes=64)
         q_bf = []
         for o in range(PASSES):
             grouped = sb.tile([P, NQ, 4], BF16, name="q_bf%d" % o, align_bytes=64)
-            nc.scalar.copy(grouped[:], q_raw[o][:].rearrange("p r q -> p q r"))
+            nc.scalar.copy(grouped[:], q_raw[:, o].rearrange("p r q -> p q r"))
             q_bf.append(grouped)
 
         def quantize(o):
             nc.vector.quantize_mx(q_codes[:, o, :].bitcast(FP8X4), q_plane[:, o, :], q_bf[o][:].rearrange("p q r -> p (q r)"))
 
-        k_codes = []
-        for b in range(BANKS):
-            picked = sb.tile([P, BANK], U32, name="picked%d" % b, align_bytes=64)
-            nc.vector.tensor_copy(picked[:], word_pool[:].bitcast(U32).indirect(offsets[:, b * BANK // 16 : (b + 1) * BANK // 16]))
-            if b == 1:
-                quantize(1)
-            parted = sb.tile([P, PASSES, BANK], U16, name="parted%d" % b, align_bytes=64)
-            nc.vector.tensor_copy(parted[:], picked[:].bitcast(U16).rearrange("p (n o) -> p o n", o=PASSES))
-            if b == 0:
-                quantize(0)
-            k_codes.append(parted)
+        picked = [sb.tile([P, BANK], U32, name="picked%d" % b, align_bytes=64) for b in range(BANKS)]
+        k_codes = [sb.tile([P, PASSES, BANK], U16, name="parted%d" % b, align_bytes=64) for b in range(BANKS)]
+
+        def gather(b):
+            nc.vector.tensor_copy(picked[b][:], word_pool[:].bitcast(U32).indirect(offsets[:, b * BANK // 16 : (b + 1) * BANK // 16]))
+
+        def part(b):
+            nc.vector.tensor_copy(k_codes[b][:], picked[b][:].bitcast(U16).rearrange("p (n o) -> p o n", o=PASSES))
+
+        gather(0)
+        part(0)
+        quantize(0)
+        gather(1)
+        quantize(1)
+        part(1)
 
         scores = []
-        for b in range(BANKS):
-            acc = psum.tile([P, BANK], F32, name="scores%d" % b)
-            for o in range(PASSES):
-                nc.tensor.matmul_mx(
-                    acc[:],
-                    lhsT=q_codes[:, o, :].bitcast(FP8X4),
-                    lhsT_scale=q_plane[:, o, :],
-                    rhs=k_codes[b][:, o, :].bitcast(FP4X4),
-                    rhs_scale=k_plane[:, o, :].bitcast(U8)[:, b * BANK : (b + 1) * BANK],
-                    start=(o == 0),
-                    stop=(o == PASSES - 1),
-                )
+        for c in range(N // PIECE):
+            acc = psum.tile([P, PIECE], F32, name="scores%d" % c)
+            for g in range(PIECE // 128):
+                lo = c * PIECE + g * 128
+                for o in range(PASSES):
+                    nc.tensor.matmul_mx(
+                        acc[:, g * 128 : (g + 1) * 128],
+                        lhsT=q_codes[:, o, :].bitcast(FP8X4),
+                        lhsT_scale=q_plane[:, o, :],
+                        rhs=k_codes[lo // BANK][:, o, lo % BANK : lo % BANK + 128].bitcast(FP4X4),
+                        rhs_scale=k_plane[:, o, :].bitcast(U8)[:, lo : lo + 128],
+                        start=(o == 0),
+                        stop=(o == PASSES - 1),
+                    )
             scores.append(acc)
 
         runs = N // SEG
@@ -105,27 +114,42 @@ def tile_attend_page_smooth_kernel(tc, qT, k_words, k_scales, offs, out):
         inv = sb.tile([P, runs], F32, name="inv")
         mean = sb.tile([P, runs], F32, name="mean")
         res = sb.tile([P, runs], F32, name="res")
-        rb = BANK // SEG
         rp = PIECE // SEG
+        per_bank = BANK // PIECE
+        pieces = N // PIECE
+
+        def runs_of(c, n=1):
+            return slice(c * rp, (c + n) * rp)
+
+        def scores_of(c):
+            return scores[c][:].rearrange("p (j s) -> p j s", s=SEG)
+
+        def total(dst, src, js):
+            nc.vector.tensor_reduce(dst[:, js], src[:, js, :], AX.X, ALU.add)
+
+        last = pieces - 1
         for b in range(BANKS):
-            a3 = scores[b][:].rearrange("p (j s) -> p j s", s=SEG)
-            halves = range(BANK // PIECE)
-            for h in halves:
-                js = slice(b * rb + h * rp, b * rb + (h + 1) * rp)
-                nc.vector.tensor_reduce(peak[:, js], a3[:, h * rp : (h + 1) * rp, :], AX.X, ALU.max)
-            for h in halves:
-                js = slice(b * rb + h * rp, b * rb + (h + 1) * rp)
-                nc.vector.tensor_tensor(below[:, js, :], a3[:, h * rp : (h + 1) * rp, :], peak[:, js].unsqueeze(2).to_broadcast([P, rp, SEG]), ALU.subtract)
+            cs = range(b * per_bank, (b + 1) * per_bank)
+            for c in cs:
+                nc.vector.tensor_reduce(peak[:, runs_of(c)], scores_of(c), AX.X, ALU.max)
+            for c in cs:
+                js = runs_of(c)
+                nc.vector.tensor_tensor(below[:, js, :], scores_of(c), peak[:, js].unsqueeze(2).to_broadcast([P, rp, SEG]), ALU.subtract)
                 nc.scalar.activation(weight[:, js, :], below[:, js, :], ACT.Exp, scale=2.0)
-                nc.gpsimd.tensor_tensor(weighted[:, js, :], below[:, js, :], weight[:, js, :], ALU.mult)
-        for b in range(BANKS):
-            js = slice(b * rb, (b + 1) * rb)
-            j0 = slice(b * rb, b * rb + rp)
-            j1 = slice(b * rb + rp, (b + 1) * rb)
-            nc.vector.tensor_reduce(den[:, js], weight[:, js, :], AX.X, ALU.add)
-            nc.vector.tensor_reduce(num[:, j0], weighted[:, j0, :], AX.X, ALU.add)
-            nc.vector.reciprocal(inv[:, js], den[:, js])
-            nc.vector.tensor_reduce(num[:, j1], weighted[:, j1, :], AX.X, ALU.add)
-        nc.vector.tensor_tensor(mean[:], num[:], inv[:], ALU.mult)
-        nc.vector.tensor_tensor(res[:], mean[:], peak[:], ALU.add)
+                if c != last:
+                    nc.gpsimd.tensor_tensor(weighted[:, js, :], below[:, js, :], weight[:, js, :], ALU.mult)
+        total(den, weight, runs_of(0, 2))
+        total(num, weighted, runs_of(0))
+        nc.vector.tensor_tensor(weighted[:, runs_of(last), :], scores_of(last), weight[:, runs_of(last), :], ALU.mult)
+        nc.vector.reciprocal(inv[:, runs_of(0, 2)], den[:, runs_of(0, 2)])
+        total(den, weight, runs_of(2, 2))
+        total(num, weighted, runs_of(1))
+        nc.vector.reciprocal(inv[:, runs_of(2, 2)], den[:, runs_of(2, 2)])
+        total(num, weighted, runs_of(2))
+        total(num, weighted, runs_of(3))
+        head = runs_of(0, last)
+        tail = runs_of(last)
+        nc.vector.tensor_tensor(mean[:, head], num[:, head], inv[:, head], ALU.mult)
+        nc.vector.tensor_tensor(res[:, tail], num[:, tail], inv[:, tail], ALU.mult)
+        nc.vector.tensor_tensor(res[:, head], mean[:, head], peak[:, head], ALU.add)
         nc.sync.dma_start(out[0], res[:])

@@ -30,7 +30,7 @@ def tile_attend_page_smooth_kernel(tc, qT, k_words, k_scales, offs, out):
         sb = ctx.enter_context(tc.tile_pool(name="sb", bufs=1))
         psum = ctx.enter_context(tc.psum_pool(name="psum", bufs=1))
 
-        scale_pool = sb.tile([P, T // 4], I32, name="scale_pool", tag="staged", align_bytes=64)
+        scale_pool = sb.tile([P, T // 4], I32, name="scale_pool", align_bytes=64)
         nc.sync.dma_start(scale_pool[0:32, :], k_scales.rearrange("o f t -> (o f) t").bitcast(I32))
         offsets = lists.tile([P, N // 16], U16, name="offsets")
         nc.sync.dma_start(offsets[:], offs)
@@ -41,6 +41,10 @@ def tile_attend_page_smooth_kernel(tc, qT, k_words, k_scales, offs, out):
         nc.sync.dma_start(word_pool[:], k_words[0].rearrange("p t b -> p (t b)").bitcast(I32))
 
 
+        q_raw = sb.tile([P, PASSES, 4, NQ], F32, name="q_raw", align_bytes=64)
+        for o in range(PASSES):
+            nc.sync.dma_start(q_raw[:, o], qT[0, 512 * o : 512 * (o + 1), :].rearrange("(p r) q -> p r q", r=4))
+
         k_plane = sb.tile([P, PASSES, N // 4], I32, name="k_plane", align_bytes=64)
         nc.vector.memset(k_plane[:], 0)
 
@@ -50,14 +54,10 @@ def tile_attend_page_smooth_kernel(tc, qT, k_words, k_scales, offs, out):
 
         def move(o, quad):
             first = 16 * o + 4 * quad
-            nc.sync.dma_start(k_plane[32 * quad : 32 * quad + 4, o, :], scale_picked[first : first + 4, :].bitcast(I32))
+            queue = nc.gpsimd if 4 * o + quad < 2 else nc.sync
+            queue.dma_start(k_plane[32 * quad : 32 * quad + 4, o, :], scale_picked[first : first + 4, :].bitcast(I32))
 
-        for o, quad in moves[:5]:
-            move(o, quad)
-        q_raw = sb.tile([P, PASSES, 4, NQ], F32, name="q_raw", tag="staged", align_bytes=64)
-        for o in range(PASSES):
-            nc.sync.dma_start(q_raw[:, o], qT[0, 512 * o : 512 * (o + 1), :].rearrange("(p r) q -> p r q", r=4))
-        for o, quad in moves[5:]:
+        for o, quad in moves:
             move(o, quad)
 
         q_codes = sb.tile([P, PASSES, NQ], U32, name="q_codes", align_bytes=64)
@@ -115,41 +115,54 @@ def tile_attend_page_smooth_kernel(tc, qT, k_words, k_scales, offs, out):
         mean = sb.tile([P, runs], F32, name="mean")
         res = sb.tile([P, runs], F32, name="res")
         rp = PIECE // SEG
-        per_bank = BANK // PIECE
-        pieces = N // PIECE
+        split = 48
+        shift = sb.tile([P, runs - split], F32, name="shift")
+        den_last = sb.tile([P, runs - split], F32, name="den_last")
 
-        def runs_of(c, n=1):
-            return slice(c * rp, (c + n) * rp)
+        def scores_of(lo, hi):
+            c = lo // rp
+            return scores[c][:].rearrange("p (j s) -> p j s", s=SEG)[:, lo - c * rp : hi - c * rp, :]
 
-        def scores_of(c):
-            return scores[c][:].rearrange("p (j s) -> p j s", s=SEG)
+        def top(lo, hi):
+            nc.vector.tensor_reduce(peak[:, lo:hi], scores_of(lo, hi), AX.X, ALU.max)
 
-        def total(dst, src, js):
-            nc.vector.tensor_reduce(dst[:, js], src[:, js, :], AX.X, ALU.add)
+        def lower(lo, hi):
+            nc.vector.tensor_tensor(below[:, lo:hi, :], scores_of(lo, hi), peak[:, lo:hi].unsqueeze(2).to_broadcast([P, hi - lo, SEG]), ALU.subtract)
 
-        last = pieces - 1
-        for b in range(BANKS):
-            cs = range(b * per_bank, (b + 1) * per_bank)
-            for c in cs:
-                nc.vector.tensor_reduce(peak[:, runs_of(c)], scores_of(c), AX.X, ALU.max)
-            for c in cs:
-                js = runs_of(c)
-                nc.vector.tensor_tensor(below[:, js, :], scores_of(c), peak[:, js].unsqueeze(2).to_broadcast([P, rp, SEG]), ALU.subtract)
-                nc.scalar.activation(weight[:, js, :], below[:, js, :], ACT.Exp, scale=2.0)
-                if c != last:
-                    nc.gpsimd.tensor_tensor(weighted[:, js, :], below[:, js, :], weight[:, js, :], ALU.mult)
-        total(den, weight, runs_of(0, 2))
-        total(num, weighted, runs_of(0))
-        nc.vector.tensor_tensor(weighted[:, runs_of(last), :], scores_of(last), weight[:, runs_of(last), :], ALU.mult)
-        nc.vector.reciprocal(inv[:, runs_of(0, 2)], den[:, runs_of(0, 2)])
-        total(den, weight, runs_of(2, 2))
-        total(num, weighted, runs_of(1))
-        nc.vector.reciprocal(inv[:, runs_of(2, 2)], den[:, runs_of(2, 2)])
-        total(num, weighted, runs_of(2))
-        total(num, weighted, runs_of(3))
-        head = runs_of(0, last)
-        tail = runs_of(last)
-        nc.vector.tensor_tensor(mean[:, head], num[:, head], inv[:, head], ALU.mult)
-        nc.vector.tensor_tensor(res[:, tail], num[:, tail], inv[:, tail], ALU.mult)
-        nc.vector.tensor_tensor(res[:, head], mean[:, head], peak[:, head], ALU.add)
+        def weigh(lo, hi):
+            nc.scalar.activation(weight[:, lo:hi, :], below[:, lo:hi, :], ACT.Exp, scale=2.0)
+            nc.gpsimd.tensor_tensor(weighted[:, lo:hi, :], below[:, lo:hi, :], weight[:, lo:hi, :], ALU.mult)
+
+        def weigh_runs(lo, hi):
+            nc.vector.tensor_scalar(shift[:, lo - split : hi - split], peak[:, lo:hi], -2.0, None, ALU.mult)
+            for j in range(lo, hi):
+                nc.scalar.activation(weight[:, j, :], scores_of(j, j + 1)[:, 0, :], ACT.Exp, bias=shift[:, j - split : j - split + 1], scale=2.0, accum_out=den_last[:, j - split : j - split + 1])
+
+        def product(lo, hi):
+            nc.vector.tensor_tensor(weighted[:, lo:hi, :], scores_of(lo, hi), weight[:, lo:hi, :], ALU.mult)
+
+        def total(dst, src, lo, hi):
+            nc.vector.tensor_reduce(dst[:, lo:hi], src[:, lo:hi, :], AX.X, ALU.add)
+
+        for lo in (0, 16, 32):
+            top(lo, lo + 8)
+            top(lo + 8, lo + 16)
+            lower(lo, lo + 8)
+            lower(lo + 8, lo + 16)
+            weigh(lo, lo + 16)
+        top(48, 64)
+        total(den, weight, 0, 16)
+        weigh_runs(48, 64)
+        total(den, weight, 16, 32)
+        total(num, weighted, 0, 16)
+        total(den, weight, 32, 48)
+        total(num, weighted, 16, 32)
+        nc.vector.reciprocal(inv[:, :split], den[:, :split])
+        total(num, weighted, 32, 48)
+        product(48, 64)
+        nc.vector.tensor_tensor(mean[:, :split], num[:, :split], inv[:, :split], ALU.mult)
+        nc.vector.reciprocal(inv[:, split:], den_last[:])
+        total(num, weighted, 48, 64)
+        nc.vector.tensor_tensor(res[:, :split], mean[:, :split], peak[:, :split], ALU.add)
+        nc.vector.tensor_tensor(res[:, split:], num[:, split:], inv[:, split:], ALU.mult)
         nc.sync.dma_start(out[0], res[:])

@@ -31,7 +31,7 @@ def tile_attend_page_smooth_kernel(tc, qT, k_words, k_scales, offs, out):
         psum = ctx.enter_context(tc.psum_pool(name="psum", bufs=1))
 
         scale_pool = sb.tile([P, T // 4], I32, name="scale_pool", align_bytes=64)
-        nc.sync.dma_start(scale_pool[0:32, :], k_scales.rearrange("o f t -> (o f) t").bitcast(I32))
+        nc.sync.dma_start(scale_pool[0:32, :], k_scales.rearrange("o f t -> f o t").bitcast(I32))
         offsets = lists.tile([P, N // 16], U16, name="offsets")
         nc.sync.dma_start(offsets[:], offs)
         nc.vector.memset(scale_pool[32:64, :], 0)
@@ -41,37 +41,32 @@ def tile_attend_page_smooth_kernel(tc, qT, k_words, k_scales, offs, out):
         nc.sync.dma_start(word_pool[:], k_words[0].rearrange("p t b -> p (t b)").bitcast(I32))
 
 
-        q_raw = sb.tile([P, PASSES, 4, NQ], F32, name="q_raw", align_bytes=64)
+        q_raw = []
         for o in range(PASSES):
-            nc.sync.dma_start(q_raw[:, o], qT[0, 512 * o : 512 * (o + 1), :].rearrange("(p r) q -> p r q", r=4))
+            raw = sb.tile([P, 4, NQ], F32, name="q_raw%d" % o, tag="stage%d" % o, align_bytes=64)
+            nc.sync.dma_start(raw[:], qT[0, 512 * o : 512 * (o + 1), :].rearrange("(p r) q -> p r q", r=4))
+            q_raw.append(raw)
 
         k_plane = sb.tile([P, PASSES, N // 4], I32, name="k_plane", align_bytes=64)
         nc.vector.memset(k_plane[:], 0)
 
         scale_picked = sb.tile([P, N], U8, name="scale_picked", align_bytes=64)
         nc.vector.tensor_copy(scale_picked[:], scale_pool[:].bitcast(U8).indirect(offsets[:]))
-        moves = [(o, quad) for o in range(PASSES) for quad in range(4)]
-
-        def move(o, quad):
-            first = 16 * o + 4 * quad
-            queue = nc.gpsimd if 4 * o + quad < 2 else nc.sync
-            queue.dma_start(k_plane[32 * quad : 32 * quad + 4, o, :], scale_picked[first : first + 4, :].bitcast(I32))
-
-        for o, quad in moves:
-            move(o, quad)
+        for quad in range(4):
+            nc.sync.dma_start(k_plane[32 * quad : 32 * quad + 4, :, :].rearrange("p o n -> p (o n)"), scale_picked[8 * quad : 8 * quad + 8, :].bitcast(I32))
 
         q_codes = sb.tile([P, PASSES, NQ], U32, name="q_codes", align_bytes=64)
         q_plane = sb.tile([P, PASSES, NQ], U8, name="q_plane", align_bytes=64)
         q_bf = []
         for o in range(PASSES):
             grouped = sb.tile([P, NQ, 4], BF16, name="q_bf%d" % o, align_bytes=64)
-            nc.scalar.copy(grouped[:], q_raw[:, o].rearrange("p r q -> p q r"))
+            nc.scalar.copy(grouped[:], q_raw[o][:].rearrange("p r q -> p q r"))
             q_bf.append(grouped)
 
         def quantize(o):
             nc.vector.quantize_mx(q_codes[:, o, :].bitcast(FP8X4), q_plane[:, o, :], q_bf[o][:].rearrange("p q r -> p (q r)"))
 
-        picked = [sb.tile([P, BANK], U32, name="picked%d" % b, align_bytes=64) for b in range(BANKS)]
+        picked = [sb.tile([P, BANK], U32, name="picked0", align_bytes=64), sb.tile([P, BANK], U32, name="picked1", tag="stage1", align_bytes=64)]
         k_codes = [sb.tile([P, PASSES, BANK], U16, name="parted%d" % b, align_bytes=64) for b in range(BANKS)]
 
         def gather(b):
@@ -83,8 +78,8 @@ def tile_attend_page_smooth_kernel(tc, qT, k_words, k_scales, offs, out):
         gather(0)
         part(0)
         quantize(0)
-        gather(1)
         quantize(1)
+        gather(1)
         part(1)
 
         scores = []

@@ -60,14 +60,14 @@ def tile_attend_page_smooth_kernel(tc, qT, k_words, k_scales, offs, out):
         q_bf = []
         for o in range(PASSES):
             grouped = sb.tile([P, NQ, 4], BF16, name="q_bf%d" % o, align_bytes=64)
-            nc.scalar.copy(grouped[:], q_raw[o][:].rearrange("p r q -> p q r"))
+            nc.scalar.copy(grouped[:].rearrange("p (c i) r -> p c r i", i=4), q_raw[o][:].rearrange("p r (c i) -> p c r i", i=4))
             q_bf.append(grouped)
 
         def quantize(o):
             nc.vector.quantize_mx(q_codes[:, o, :].bitcast(FP8X4), q_plane[:, o, :], q_bf[o][:].rearrange("p q r -> p (q r)"))
 
-        picked = [sb.tile([P, BANK], U32, name="picked0", align_bytes=64), sb.tile([P, BANK], U32, name="picked1", tag="stage1", align_bytes=64)]
-        k_codes = [sb.tile([P, PASSES, BANK], U16, name="parted%d" % b, align_bytes=64) for b in range(BANKS)]
+        picked = [sb.tile([P, BANK], U32, name="picked%d" % b, align_bytes=64) for b in range(BANKS)]
+        k_codes = [sb.tile([P, PASSES, BANK], U16, name="parted0", align_bytes=64), sb.tile([P, PASSES, BANK], U16, name="parted1", tag="stage1", align_bytes=64)]
 
         def gather(b):
             nc.vector.tensor_copy(picked[b][:], word_pool[:].bitcast(U32).indirect(offsets[:, b * BANK // 16 : (b + 1) * BANK // 16]))
@@ -77,27 +77,31 @@ def tile_attend_page_smooth_kernel(tc, qT, k_words, k_scales, offs, out):
 
         gather(0)
         part(0)
+        gather(1)
         quantize(0)
         quantize(1)
-        gather(1)
         part(1)
 
-        scores = []
-        for c in range(N // PIECE):
+        def multiply(acc, lo, width):
+            for o in range(PASSES):
+                nc.tensor.matmul_mx(
+                    acc,
+                    lhsT=q_codes[:, o, :].bitcast(FP8X4),
+                    lhsT_scale=q_plane[:, o, :],
+                    rhs=k_codes[lo // BANK][:, o, lo % BANK : lo % BANK + width].bitcast(FP4X4),
+                    rhs_scale=k_plane[:, o, :].bitcast(U8)[:, lo : lo + width],
+                    start=(o == 0),
+                    stop=(o == PASSES - 1),
+                )
+
+        first = psum.tile([P, BANK], F32, name="first")
+        multiply(first[:], 0, BANK)
+        scores = [first[:, 0:PIECE], first[:, PIECE:BANK]]
+        for c in (2, 3):
             acc = psum.tile([P, PIECE], F32, name="scores%d" % c)
             for g in range(PIECE // 128):
-                lo = c * PIECE + g * 128
-                for o in range(PASSES):
-                    nc.tensor.matmul_mx(
-                        acc[:, g * 128 : (g + 1) * 128],
-                        lhsT=q_codes[:, o, :].bitcast(FP8X4),
-                        lhsT_scale=q_plane[:, o, :],
-                        rhs=k_codes[lo // BANK][:, o, lo % BANK : lo % BANK + 128].bitcast(FP4X4),
-                        rhs_scale=k_plane[:, o, :].bitcast(U8)[:, lo : lo + 128],
-                        start=(o == 0),
-                        stop=(o == PASSES - 1),
-                    )
-            scores.append(acc)
+                multiply(acc[:, g * 128 : (g + 1) * 128], c * PIECE + g * 128, 128)
+            scores.append(acc[:])
 
         runs = N // SEG
         peak = sb.tile([P, runs], F32, name="peak")
@@ -116,10 +120,10 @@ def tile_attend_page_smooth_kernel(tc, qT, k_words, k_scales, offs, out):
 
         def scores_of(lo, hi):
             c = lo // rp
-            return scores[c][:].rearrange("p (j s) -> p j s", s=SEG)[:, lo - c * rp : hi - c * rp, :]
+            return scores[c].rearrange("p (j s) -> p j s", s=SEG)[:, lo - c * rp : hi - c * rp, :]
 
         def top(lo, hi):
-            nc.vector.tensor_reduce(peak[:, lo:hi], scores_of(lo, hi), AX.X, ALU.max)
+            nc.vector.tensor_reduce(peak[:, lo:hi], scores_of(lo, hi), AX.X, ALU.max, negate=(lo >= split))
 
         def lower(lo, hi):
             nc.vector.tensor_tensor(below[:, lo:hi, :], scores_of(lo, hi), peak[:, lo:hi].unsqueeze(2).to_broadcast([P, hi - lo, SEG]), ALU.subtract)
@@ -129,7 +133,7 @@ def tile_attend_page_smooth_kernel(tc, qT, k_words, k_scales, offs, out):
             nc.gpsimd.tensor_tensor(weighted[:, lo:hi, :], below[:, lo:hi, :], weight[:, lo:hi, :], ALU.mult)
 
         def weigh_runs(lo, hi):
-            nc.vector.tensor_scalar(shift[:, lo - split : hi - split], peak[:, lo:hi], -2.0, None, ALU.mult)
+            nc.vector.tensor_reduce(shift[:, lo - split : hi - split], peak[:, lo:hi].unsqueeze(2).to_broadcast([P, hi - lo, 2]), AX.X, ALU.add)
             for j in range(lo, hi):
                 nc.scalar.activation(weight[:, j, :], scores_of(j, j + 1)[:, 0, :], ACT.Exp, bias=shift[:, j - split : j - split + 1], scale=2.0, accum_out=den_last[:, j - split : j - split + 1])
 
@@ -139,13 +143,16 @@ def tile_attend_page_smooth_kernel(tc, qT, k_words, k_scales, offs, out):
         def total(dst, src, lo, hi):
             nc.vector.tensor_reduce(dst[:, lo:hi], src[:, lo:hi, :], AX.X, ALU.add)
 
-        for lo in (0, 16, 32):
-            top(lo, lo + 8)
-            top(lo + 8, lo + 16)
-            lower(lo, lo + 8)
-            lower(lo + 8, lo + 16)
-            weigh(lo, lo + 16)
+        top(0, 16)
+        top(16, 32)
+        lower(0, 16)
+        lower(16, 32)
+        weigh(0, 16)
+        weigh(16, 32)
+        top(32, 48)
         top(48, 64)
+        lower(32, 48)
+        weigh(32, 48)
         total(den, weight, 0, 16)
         weigh_runs(48, 64)
         total(den, weight, 16, 32)

@@ -52,7 +52,7 @@ def tile_attend_page_smooth_kernel(tc, qT, k_words, k_scales, offs, out):
 
         scale_picked = sb.tile([P, N], U8, name="scale_picked", align_bytes=64)
         nc.vector.tensor_copy(scale_picked[:], scale_pool[:].bitcast(U8).indirect(offsets[:]))
-        for quad in range(4):
+        for quad in (0, 2, 1, 3):
             nc.sync.dma_start(k_plane[32 * quad : 32 * quad + 4, :, :].rearrange("p o n -> p (o n)"), scale_picked[8 * quad : 8 * quad + 8, :].bitcast(I32))
 
         q_codes = sb.tile([P, PASSES, NQ], U32, name="q_codes", align_bytes=64)
@@ -66,7 +66,7 @@ def tile_attend_page_smooth_kernel(tc, qT, k_words, k_scales, offs, out):
         def quantize(o):
             nc.vector.quantize_mx(q_codes[:, o, :].bitcast(FP8X4), q_plane[:, o, :], q_bf[o][:].rearrange("p q r -> p (q r)"))
 
-        picked = [sb.tile([P, BANK], U32, name="picked%d" % b, align_bytes=64) for b in range(BANKS)]
+        picked = [sb.tile([P, BANK], U32, name="picked0", align_bytes=64), sb.tile([P, BANK], U32, name="picked1", tag="stage0", align_bytes=64)]
         k_codes = [sb.tile([P, PASSES, BANK], U16, name="parted0", align_bytes=64), sb.tile([P, PASSES, BANK], U16, name="parted1", tag="stage1", align_bytes=64)]
 
         def gather(b):
@@ -77,8 +77,8 @@ def tile_attend_page_smooth_kernel(tc, qT, k_words, k_scales, offs, out):
 
         gather(0)
         part(0)
-        gather(1)
         quantize(0)
+        gather(1)
         quantize(1)
         part(1)
 

@@ -66,42 +66,52 @@ def tile_attend_page_smooth_kernel(tc, qT, k_words, k_scales, offs, out):
         def quantize(o):
             nc.vector.quantize_mx(q_codes[:, o, :].bitcast(FP8X4), q_plane[:, o, :], q_bf[o][:].rearrange("p q r -> p (q r)"))
 
-        picked = [sb.tile([P, BANK], U32, name="picked0", align_bytes=64), sb.tile([P, BANK], U32, name="picked1", tag="stage0", align_bytes=64)]
-        k_codes = [sb.tile([P, PASSES, BANK], U16, name="parted0", align_bytes=64), sb.tile([P, PASSES, BANK], U16, name="parted1", tag="stage1", align_bytes=64)]
+        picked = [sb.tile([P, BANK], U32, name="picked%d" % b, align_bytes=64) for b in range(BANKS)]
+        k_codes = [
+            sb.tile([P, PASSES, PIECE], U16, name="parted0", align_bytes=64)[:],
+            sb.tile([P, PASSES, PIECE], U16, name="parted1", tag="stage0", align_bytes=64)[:],
+        ]
+        late = sb.tile([P, 2, PASSES, PIECE], U16, name="parted_late", tag="stage1", align_bytes=64)
+        k_codes = k_codes + [late[:, 0], late[:, 1]]
 
         def gather(b):
             nc.vector.tensor_copy(picked[b][:], word_pool[:].bitcast(U32).indirect(offsets[:, b * BANK // 16 : (b + 1) * BANK // 16]))
 
-        def part(b):
-            nc.vector.tensor_copy(k_codes[b][:], picked[b][:].bitcast(U16).rearrange("p (n o) -> p o n", o=PASSES))
+        def part(c):
+            words = picked[c // 2][:, (c % 2) * PIECE : (c % 2 + 1) * PIECE]
+            nc.vector.tensor_copy(k_codes[c], words.bitcast(U16).rearrange("p (n o) -> p o n", o=PASSES))
 
         gather(0)
+        gather(1)
         part(0)
         quantize(0)
-        gather(1)
-        quantize(1)
         part(1)
+        quantize(1)
+        part(2)
+        part(3)
 
-        def multiply(acc, lo, width):
-            for o in range(PASSES):
-                nc.tensor.matmul_mx(
-                    acc,
-                    lhsT=q_codes[:, o, :].bitcast(FP8X4),
-                    lhsT_scale=q_plane[:, o, :],
-                    rhs=k_codes[lo // BANK][:, o, lo % BANK : lo % BANK + width].bitcast(FP4X4),
-                    rhs_scale=k_plane[:, o, :].bitcast(U8)[:, lo : lo + width],
-                    start=(o == 0),
-                    stop=(o == PASSES - 1),
-                )
+        def multiply(acc, lo, o):
+            nc.tensor.matmul_mx(
+                acc,
+                lhsT=q_codes[:, o, :].bitcast(FP8X4),
+                lhsT_scale=q_plane[:, o, :],
+                rhs=k_codes[lo // PIECE][:, o, lo % PIECE : lo % PIECE + 128].bitcast(FP4X4),
+                rhs_scale=k_plane[:, o, :].bitcast(U8)[:, lo : lo + 128],
+                start=(o == 0),
+                stop=(o == PASSES - 1),
+            )
 
-        first = psum.tile([P, BANK], F32, name="first")
-        multiply(first[:], 0, BANK)
-        scores = [first[:, 0:PIECE], first[:, PIECE:BANK]]
-        for c in (2, 3):
-            acc = psum.tile([P, PIECE], F32, name="scores%d" % c)
-            for g in range(PIECE // 128):
-                multiply(acc[:, g * 128 : (g + 1) * 128], c * PIECE + g * 128, 128)
-            scores.append(acc[:])
+        first = [psum.tile([P, 128], F32, name="first%d" % g) for g in range(4)]
+        for o in range(PASSES):
+            for g in range(4):
+                multiply(first[g][:], g * 128, o)
+        scores = {8 * g: first[g][:] for g in range(4)}
+        for lo, width in ((512, 256), (768, 128), (896, 128)):
+            acc = psum.tile([P, width], F32, name="scores%d" % lo)
+            for g in range(width // 128):
+                for o in range(PASSES):
+                    multiply(acc[:, g * 128 : (g + 1) * 128], lo + g * 128, o)
+            scores[lo // SEG] = acc[:]
 
         runs = N // SEG
         peak = sb.tile([P, runs], F32, name="peak")
@@ -113,14 +123,13 @@ def tile_attend_page_smooth_kernel(tc, qT, k_words, k_scales, offs, out):
         inv = sb.tile([P, runs], F32, name="inv")
         mean = sb.tile([P, runs], F32, name="mean")
         res = sb.tile([P, runs], F32, name="res")
-        rp = PIECE // SEG
         split = 48
         shift = sb.tile([P, runs - split], F32, name="shift")
         den_last = sb.tile([P, runs - split], F32, name="den_last")
 
         def scores_of(lo, hi):
-            c = lo // rp
-            return scores[c].rearrange("p (j s) -> p j s", s=SEG)[:, lo - c * rp : hi - c * rp, :]
+            at = max(a for a in scores if a <= lo)
+            return scores[at].rearrange("p (j s) -> p j s", s=SEG)[:, lo - at : hi - at, :]
 
         def top(lo, hi):
             nc.vector.tensor_reduce(peak[:, lo:hi], scores_of(lo, hi), AX.X, ALU.max, negate=(lo >= split))
@@ -143,15 +152,16 @@ def tile_attend_page_smooth_kernel(tc, qT, k_words, k_scales, offs, out):
         def total(dst, src, lo, hi):
             nc.vector.tensor_reduce(dst[:, lo:hi], src[:, lo:hi, :], AX.X, ALU.add)
 
-        top(0, 16)
-        top(16, 32)
-        lower(0, 16)
-        lower(16, 32)
-        weigh(0, 16)
-        weigh(16, 32)
+        for lo in (0, 16):
+            top(lo, lo + 8)
+            top(lo + 8, lo + 16)
+            lower(lo, lo + 8)
+            lower(lo + 8, lo + 16)
+            weigh(lo, lo + 16)
         top(32, 48)
-        top(48, 64)
+        top(48, 56)
         lower(32, 48)
+        top(56, 64)
         weigh(32, 48)
         total(den, weight, 0, 16)
         weigh_runs(48, 64)
@@ -160,11 +170,13 @@ def tile_attend_page_smooth_kernel(tc, qT, k_words, k_scales, offs, out):
         total(den, weight, 32, 48)
         total(num, weighted, 16, 32)
         nc.vector.reciprocal(inv[:, :split], den[:, :split])
+        product(48, 56)
         total(num, weighted, 32, 48)
-        product(48, 64)
-        nc.vector.tensor_tensor(mean[:, :split], num[:, :split], inv[:, :split], ALU.mult)
+        product(56, 64)
+        total(num, weighted, 48, 56)
         nc.vector.reciprocal(inv[:, split:], den_last[:])
-        total(num, weighted, 48, 64)
-        nc.vector.tensor_tensor(res[:, :split], mean[:, :split], peak[:, :split], ALU.add)
+        total(num, weighted, 56, 64)
+        nc.vector.tensor_tensor(mean[:, :split], num[:, :split], inv[:, :split], ALU.mult)
         nc.vector.tensor_tensor(res[:, split:], num[:, split:], inv[:, split:], ALU.mult)
+        nc.vector.tensor_tensor(res[:, :split], mean[:, :split], peak[:, :split], ALU.add)
         nc.sync.dma_start(out[0], res[:])

@@ -44,7 +44,7 @@ def tile_attend_page_smooth_kernel(tc, qT, k_words, k_scales, offs, out):
         q_raw = []
         for o in range(PASSES):
             raw = sb.tile([P, 4, NQ], F32, name="q_raw%d" % o, tag="stage%d" % o, align_bytes=64)
-            nc.sync.dma_start(raw[:], qT[0, 512 * o : 512 * (o + 1), :].rearrange("(p r) q -> p r q", r=4))
+            nc.sync.dma_start(raw[:].rearrange("p r q -> p (r q)"), qT[0, 512 * o : 512 * (o + 1), :].rearrange("(p r) q -> p (r q)", r=4))
             q_raw.append(raw)
 
         k_plane = sb.tile([P, PASSES, N // 4], I32, name="k_plane", align_bytes=64)
@@ -67,12 +67,13 @@ def tile_attend_page_smooth_kernel(tc, qT, k_words, k_scales, offs, out):
             nc.vector.quantize_mx(q_codes[:, o, :].bitcast(FP8X4), q_plane[:, o, :], q_bf[o][:].rearrange("p q r -> p (q r)"))
 
         picked = [sb.tile([P, BANK], U32, name="picked%d" % b, align_bytes=64) for b in range(BANKS)]
+        middle = sb.tile([P, 2, PASSES, PIECE], U16, name="parted_middle", tag="stage0", align_bytes=64)
         k_codes = [
             sb.tile([P, PASSES, PIECE], U16, name="parted0", align_bytes=64)[:],
-            sb.tile([P, PASSES, PIECE], U16, name="parted1", tag="stage0", align_bytes=64)[:],
+            middle[:, 0],
+            middle[:, 1],
+            sb.tile([P, PASSES, PIECE], U16, name="parted3", tag="stage1", align_bytes=64)[:],
         ]
-        late = sb.tile([P, 2, PASSES, PIECE], U16, name="parted_late", tag="stage1", align_bytes=64)
-        k_codes = k_codes + [late[:, 0], late[:, 1]]
 
         def gather(b):
             nc.vector.tensor_copy(picked[b][:], word_pool[:].bitcast(U32).indirect(offsets[:, b * BANK // 16 : (b + 1) * BANK // 16]))
@@ -86,8 +87,8 @@ def tile_attend_page_smooth_kernel(tc, qT, k_words, k_scales, offs, out):
         part(0)
         quantize(0)
         part(1)
-        quantize(1)
         part(2)
+        quantize(1)
         part(3)
 
         def multiply(acc, lo, o):

@@ -19,7 +19,6 @@ N, T, D, NQ, SEG = 1024, 4096, 1024, 128, 16
 PASSES = 2
 BANK = 512
 BANKS = N // BANK
-PIECE = 256
 FLOPS = 2 * NQ * D * N
 
 
@@ -30,12 +29,11 @@ def tile_attend_page_smooth_kernel(tc, qT, k_words, k_scales, offs, out):
         sb = ctx.enter_context(tc.tile_pool(name="sb", bufs=1))
         psum = ctx.enter_context(tc.psum_pool(name="psum", bufs=1))
 
-        scale_pool = sb.tile([P, T // 4], I32, name="scale_pool", align_bytes=64)
-        nc.sync.dma_start(scale_pool[0:32, :], k_scales.rearrange("o f t -> f o t").bitcast(I32))
+        scale_pool = sb.tile([P, T // 4], I32, name="scale_pool", tag="scale_pool", align_bytes=64)
+        nc.sync.dma_start(scale_pool[96:128, :], k_scales.rearrange("o f t -> f o t").bitcast(I32))
         offsets = lists.tile([P, N // 16], U16, name="offsets")
         nc.sync.dma_start(offsets[:], offs)
-        nc.vector.memset(scale_pool[32:64, :], 0)
-        nc.gpsimd.memset(scale_pool[64:128, :], 0)
+        nc.gpsimd.memset(scale_pool[0:96, :], 0)
 
         word_pool = sb.tile([P, T], I32, name="word_pool", align_bytes=64)
         nc.sync.dma_start(word_pool[:], k_words[0].rearrange("p t b -> p (t b)").bitcast(I32))
@@ -47,56 +45,61 @@ def tile_attend_page_smooth_kernel(tc, qT, k_words, k_scales, offs, out):
             nc.sync.dma_start(raw[:].rearrange("p r q -> p (r q)"), qT[0, 512 * o : 512 * (o + 1), :].rearrange("(p r) q -> p (r q)", r=4))
             q_raw.append(raw)
 
-        k_plane = sb.tile([P, PASSES, N // 4], I32, name="k_plane", align_bytes=64)
-        nc.vector.memset(k_plane[:], 0)
-
         scale_picked = sb.tile([P, N], U8, name="scale_picked", align_bytes=64)
         nc.vector.tensor_copy(scale_picked[:], scale_pool[:].bitcast(U8).indirect(offsets[:]))
+        k_plane = sb.tile([P, PASSES, N // 4], I32, name="k_plane", tag="scale_pool", align_bytes=64)
         for quad in (0, 2, 1, 3):
-            nc.sync.dma_start(k_plane[32 * quad : 32 * quad + 4, :, :].rearrange("p o n -> p (o n)"), scale_picked[8 * quad : 8 * quad + 8, :].bitcast(I32))
+            nc.sync.dma_start(k_plane[32 * quad : 32 * quad + 4, :, :].rearrange("p o n -> p (o n)"), scale_picked[96 + 8 * quad : 96 + 8 * quad + 8, :].bitcast(I32))
 
         q_codes = sb.tile([P, PASSES, NQ], U32, name="q_codes", align_bytes=64)
         q_plane = sb.tile([P, PASSES, NQ], U8, name="q_plane", align_bytes=64)
         q_bf = []
+        q_cuts = (((0, NQ),), ((0, NQ // 2), (NQ // 2, NQ)))
         for o in range(PASSES):
             grouped = sb.tile([P, NQ, 4], BF16, name="q_bf%d" % o, align_bytes=64)
-            nc.scalar.copy(grouped[:].rearrange("p (c i) r -> p c r i", i=4), q_raw[o][:].rearrange("p r (c i) -> p c r i", i=4))
+            for lo, hi in q_cuts[o]:
+                nc.scalar.copy(grouped[:, lo:hi, :].rearrange("p (c i) r -> p c r i", i=4), q_raw[o][:, :, lo:hi].rearrange("p r (c i) -> p c r i", i=4))
             q_bf.append(grouped)
 
         def quantize(o):
-            nc.vector.quantize_mx(q_codes[:, o, :].bitcast(FP8X4), q_plane[:, o, :], q_bf[o][:].rearrange("p q r -> p (q r)"))
+            for lo, hi in q_cuts[o]:
+                nc.vector.quantize_mx(q_codes[:, o, lo:hi].bitcast(FP8X4), q_plane[:, o, lo:hi], q_bf[o][:, lo:hi, :].rearrange("p q r -> p (q r)"))
 
         picked = [sb.tile([P, BANK], U32, name="picked%d" % b, align_bytes=64) for b in range(BANKS)]
-        middle = sb.tile([P, 2, PASSES, PIECE], U16, name="parted_middle", tag="stage0", align_bytes=64)
-        k_codes = [
-            sb.tile([P, PASSES, PIECE], U16, name="parted0", align_bytes=64)[:],
-            middle[:, 0],
-            middle[:, 1],
-            sb.tile([P, PASSES, PIECE], U16, name="parted3", tag="stage1", align_bytes=64)[:],
-        ]
+        middle = sb.tile([P, PASSES * 384], U16, name="parted_middle", tag="stage0", align_bytes=64)
+        pieces = {
+            (0, 256): sb.tile([P, PASSES, 256], U16, name="parted0", align_bytes=64)[:],
+            (256, 512): middle[:, : PASSES * 256].rearrange("p (o n) -> p o n", o=PASSES),
+            (512, 640): middle[:, PASSES * 256 :].rearrange("p (o n) -> p o n", o=PASSES),
+            (640, 1024): sb.tile([P, PASSES, 384], U16, name="parted3", tag="stage1", align_bytes=64)[:],
+        }
 
         def gather(b):
             nc.vector.tensor_copy(picked[b][:], word_pool[:].bitcast(U32).indirect(offsets[:, b * BANK // 16 : (b + 1) * BANK // 16]))
 
-        def part(c):
-            words = picked[c // 2][:, (c % 2) * PIECE : (c % 2 + 1) * PIECE]
-            nc.vector.tensor_copy(k_codes[c], words.bitcast(U16).rearrange("p (n o) -> p o n", o=PASSES))
+        def part(lo, hi):
+            words = picked[lo // BANK][:, lo % BANK : lo % BANK + hi - lo]
+            nc.vector.tensor_copy(pieces[lo, hi], words.bitcast(U16).rearrange("p (n o) -> p o n", o=PASSES))
+
+        def codes_of(at, o):
+            lo, hi = max(piece for piece in pieces if piece[0] <= at)
+            return pieces[lo, hi][:, o, at - lo : at - lo + 128]
 
         gather(0)
         gather(1)
-        part(0)
+        part(0, 256)
         quantize(0)
-        part(1)
-        part(2)
+        part(256, 512)
+        part(512, 640)
         quantize(1)
-        part(3)
+        part(640, 1024)
 
         def multiply(acc, lo, o):
             nc.tensor.matmul_mx(
                 acc,
                 lhsT=q_codes[:, o, :].bitcast(FP8X4),
                 lhsT_scale=q_plane[:, o, :],
-                rhs=k_codes[lo // PIECE][:, o, lo % PIECE : lo % PIECE + 128].bitcast(FP4X4),
+                rhs=codes_of(lo, o).bitcast(FP4X4),
                 rhs_scale=k_plane[:, o, :].bitcast(U8)[:, lo : lo + 128],
                 start=(o == 0),
                 stop=(o == PASSES - 1),

@@ -30,10 +30,11 @@ def tile_attend_page_smooth_kernel(tc, qT, k_words, k_scales, offs, out):
         psum = ctx.enter_context(tc.psum_pool(name="psum", bufs=1))
 
         scale_pool = sb.tile([P, T // 4], I32, name="scale_pool", tag="scale_pool", align_bytes=64)
-        nc.sync.dma_start(scale_pool[96:128, :], k_scales.rearrange("o f t -> f o t").bitcast(I32))
+        nc.sync.dma_start(scale_pool[0:32, :], k_scales.rearrange("o f t -> f o t").bitcast(I32))
         offsets = lists.tile([P, N // 16], U16, name="offsets")
         nc.sync.dma_start(offsets[:], offs)
-        nc.gpsimd.memset(scale_pool[0:96, :], 0)
+        nc.vector.memset(scale_pool[32:64, :], 0)
+        nc.gpsimd.memset(scale_pool[64:128, :], 0)
 
         word_pool = sb.tile([P, T], I32, name="word_pool", align_bytes=64)
         nc.sync.dma_start(word_pool[:], k_words[0].rearrange("p t b -> p (t b)").bitcast(I32))
@@ -49,7 +50,7 @@ def tile_attend_page_smooth_kernel(tc, qT, k_words, k_scales, offs, out):
         nc.vector.tensor_copy(scale_picked[:], scale_pool[:].bitcast(U8).indirect(offsets[:]))
         k_plane = sb.tile([P, PASSES, N // 4], I32, name="k_plane", tag="scale_pool", align_bytes=64)
         for quad in (0, 2, 1, 3):
-            nc.sync.dma_start(k_plane[32 * quad : 32 * quad + 4, :, :].rearrange("p o n -> p (o n)"), scale_picked[96 + 8 * quad : 96 + 8 * quad + 8, :].bitcast(I32))
+            nc.sync.dma_start(k_plane[32 * quad : 32 * quad + 4, :, :].rearrange("p o n -> p (o n)"), scale_picked[8 * quad : 8 * quad + 8, :].bitcast(I32))
 
         q_codes = sb.tile([P, PASSES, NQ], U32, name="q_codes", align_bytes=64)
         q_plane = sb.tile([P, PASSES, NQ], U8, name="q_plane", align_bytes=64)

from contextlib import ExitStack

import concourse.mybir as mybir

F32 = mybir.dt.float32
BF16 = mybir.dt.bfloat16
I32 = mybir.dt.int32
U32 = mybir.dt.uint32
U16 = mybir.dt.uint16
U8 = mybir.dt.uint8
FP8X4 = mybir.dt.float8_e4m3fn_x4
FP4X4 = mybir.dt.float4_e2m1fn_x4
ALU = mybir.AluOpType
ACT = mybir.ActivationFunctionType
AX = mybir.AxisListType

P = 128
N, T, D, NQ, SEG = 1024, 4096, 1024, 128, 16
PASSES = 2
BANK = 512
BANKS = N // BANK
FLOPS = 2 * NQ * D * N


def tile_attend_page_smooth_kernel(tc, qT, k_words, k_scales, offs, out):
    nc = tc.nc
    with ExitStack() as ctx:
        lists = ctx.enter_context(tc.tile_pool(name="lists", bufs=1))
        sb = ctx.enter_context(tc.tile_pool(name="sb", bufs=1))
        psum = ctx.enter_context(tc.psum_pool(name="psum", bufs=1))

        scale_pool = sb.tile([P, T // 4], I32, name="scale_pool", tag="scale_pool", align_bytes=64)
        nc.sync.dma_start(scale_pool[0:32, :], k_scales.rearrange("o f t -> f o t").bitcast(I32))
        offsets = lists.tile([P, N // 16], U16, name="offsets")
        nc.sync.dma_start(offsets[:], offs)
        nc.vector.memset(scale_pool[32:64, :], 0)
        nc.gpsimd.memset(scale_pool[64:128, :], 0)

        word_pool = sb.tile([P, T], I32, name="word_pool", align_bytes=64)
        nc.sync.dma_start(word_pool[:], k_words[0].rearrange("p t b -> p (t b)").bitcast(I32))


        q_raw = []
        for o in range(PASSES):
            raw = sb.tile([P, 4, NQ], F32, name="q_raw%d" % o, tag="stage%d" % o, align_bytes=64)
            nc.sync.dma_start(raw[:].rearrange("p r q -> p (r q)"), qT[0, 512 * o : 512 * (o + 1), :].rearrange("(p r) q -> p (r q)", r=4))
            q_raw.append(raw)

        scale_picked = sb.tile([P, N], U8, name="scale_picked", align_bytes=64)
        nc.vector.tensor_copy(scale_picked[:], scale_pool[:].bitcast(U8).indirect(offsets[:]))
        k_plane = sb.tile([P, PASSES, N // 4], I32, name="k_plane", tag="scale_pool", align_bytes=64)
        for quad in (0, 2, 1, 3):
            nc.sync.dma_start(k_plane[32 * quad : 32 * quad + 4, :, :].rearrange("p o n -> p (o n)"), scale_picked[8 * quad : 8 * quad + 8, :].bitcast(I32))

        q_codes = sb.tile([P, PASSES, NQ], U32, name="q_codes", align_bytes=64)
        q_plane = sb.tile([P, PASSES, NQ], U8, name="q_plane", align_bytes=64)
        q_bf = []
        q_cuts = (((0, NQ),), ((0, NQ // 2), (NQ // 2, NQ)))
        for o in range(PASSES):
            grouped = sb.tile([P, NQ, 4], BF16, name="q_bf%d" % o, align_bytes=64)
            for lo, hi in q_cuts[o]:
                nc.scalar.copy(grouped[:, lo:hi, :].rearrange("p (c i) r -> p c r i", i=4), q_raw[o][:, :, lo:hi].rearrange("p r (c i) -> p c r i", i=4))
            q_bf.append(grouped)

        def quantize(o):
            for lo, hi in q_cuts[o]:
                nc.vector.quantize_mx(q_codes[:, o, lo:hi].bitcast(FP8X4), q_plane[:, o, lo:hi], q_bf[o][:, lo:hi, :].rearrange("p q r -> p (q r)"))

        picked = [sb.tile([P, BANK], U32, name="picked%d" % b, align_bytes=64) for b in range(BANKS)]
        middle = sb.tile([P, PASSES * 384], U16, name="parted_middle", tag="stage0", align_bytes=64)
        pieces = {
            (0, 256): sb.tile([P, PASSES, 256], U16, name="parted0", align_bytes=64)[:],
            (256, 512): middle[:, : PASSES * 256].rearrange("p (o n) -> p o n", o=PASSES),
            (512, 640): middle[:, PASSES * 256 :].rearrange("p (o n) -> p o n", o=PASSES),
            (640, 1024): sb.tile([P, PASSES, 384], U16, name="parted3", tag="stage1", align_bytes=64)[:],
        }

        def gather(b):
            nc.vector.tensor_copy(picked[b][:], word_pool[:].bitcast(U32).indirect(offsets[:, b * BANK // 16 : (b + 1) * BANK // 16]))

        def part(lo, hi):
            words = picked[lo // BANK][:, lo % BANK : lo % BANK + hi - lo]
            nc.vector.tensor_copy(pieces[lo, hi], words.bitcast(U16).rearrange("p (n o) -> p o n", o=PASSES))

        def codes_of(at, o):
            lo, hi = max(piece for piece in pieces if piece[0] <= at)
            return pieces[lo, hi][:, o, at - lo : at - lo + 128]

        gather(0)
        gather(1)
        part(0, 256)
        quantize(0)
        part(256, 512)
        part(512, 640)
        quantize(1)
        part(640, 1024)

        def multiply(acc, lo, o):
            nc.tensor.matmul_mx(
                acc,
                lhsT=q_codes[:, o, :].bitcast(FP8X4),
                lhsT_scale=q_plane[:, o, :],
                rhs=codes_of(lo, o).bitcast(FP4X4),
                rhs_scale=k_plane[:, o, :].bitcast(U8)[:, lo : lo + 128],
                start=(o == 0),
                stop=(o == PASSES - 1),
            )

        first = [psum.tile([P, 128], F32, name="first%d" % g) for g in range(4)]
        for o in range(PASSES):
            for g in range(4):
                multiply(first[g][:], g * 128, o)
        scores = {8 * g: first[g][:] for g in range(4)}
        for lo, width in ((512, 256), (768, 128), (896, 128)):
            acc = psum.tile([P, width], F32, name="scores%d" % lo)
            for g in range(width // 128):
                for o in range(PASSES):
                    multiply(acc[:, g * 128 : (g + 1) * 128], lo + g * 128, o)
            scores[lo // SEG] = acc[:]

        runs = N // SEG
        peak = sb.tile([P, runs], F32, name="peak")
        below = sb.tile([P, runs, SEG], F32, name="below")
        weight = sb.tile([P, runs, SEG], F32, name="weight")
        weighted = sb.tile([P, runs, SEG], F32, name="weighted")
        den = sb.tile([P, runs], F32, name="den")
        num = sb.tile([P, runs], F32, name="num")
        inv = sb.tile([P, runs], F32, name="inv")
        mean = sb.tile([P, runs], F32, name="mean")
        res = sb.tile([P, runs], F32, name="res")
        split = 48
        shift = sb.tile([P, runs - split], F32, name="shift")
        den_last = sb.tile([P, runs - split], F32, name="den_last")

        def scores_of(lo, hi):
            at = max(a for a in scores if a <= lo)
            return scores[at].rearrange("p (j s) -> p j s", s=SEG)[:, lo - at : hi - at, :]

        def top(lo, hi):
            nc.vector.tensor_reduce(peak[:, lo:hi], scores_of(lo, hi), AX.X, ALU.max, negate=(lo >= split))

        def lower(lo, hi):
            nc.vector.tensor_tensor(below[:, lo:hi, :], scores_of(lo, hi), peak[:, lo:hi].unsqueeze(2).to_broadcast([P, hi - lo, SEG]), ALU.subtract)

        def weigh(lo, hi):
            nc.scalar.activation(weight[:, lo:hi, :], below[:, lo:hi, :], ACT.Exp, scale=2.0)
            nc.gpsimd.tensor_tensor(weighted[:, lo:hi, :], below[:, lo:hi, :], weight[:, lo:hi, :], ALU.mult)

        def weigh_runs(lo, hi):
            nc.vector.tensor_reduce(shift[:, lo - split : hi - split], peak[:, lo:hi].unsqueeze(2).to_broadcast([P, hi - lo, 2]), AX.X, ALU.add)
            for j in range(lo, hi):
                nc.scalar.activation(weight[:, j, :], scores_of(j, j + 1)[:, 0, :], ACT.Exp, bias=shift[:, j - split : j - split + 1], scale=2.0, accum_out=den_last[:, j - split : j - split + 1])

        def product(lo, hi):
            nc.vector.tensor_tensor(weighted[:, lo:hi, :], scores_of(lo, hi), weight[:, lo:hi, :], ALU.mult)

        def total(dst, src, lo, hi):
            nc.vector.tensor_reduce(dst[:, lo:hi], src[:, lo:hi, :], AX.X, ALU.add)

        for lo in (0, 16):
            top(lo, lo + 8)
            top(lo + 8, lo + 16)
            lower(lo, lo + 8)
            lower(lo + 8, lo + 16)
            weigh(lo, lo + 16)
        top(32, 48)
        top(48, 56)
        lower(32, 48)
        top(56, 64)
        weigh(32, 48)
        total(den, weight, 0, 16)
        weigh_runs(48, 64)
        total(den, weight, 16, 32)
        total(num, weighted, 0, 16)
        total(den, weight, 32, 48)
        total(num, weighted, 16, 32)
        nc.vector.reciprocal(inv[:, :split], den[:, :split])
        product(48, 56)
        total(num, weighted, 32, 48)
        product(56, 64)
        total(num, weighted, 48, 56)
        nc.vector.reciprocal(inv[:, split:], den_last[:])
        total(num, weighted, 56, 64)
        nc.vector.tensor_tensor(mean[:, :split], num[:, :split], inv[:, :split], ALU.mult)
        nc.vector.tensor_tensor(res[:, split:], num[:, split:], inv[:, split:], ALU.mult)
        nc.vector.tensor_tensor(res[:, :split], mean[:, :split], peak[:, :split], ALU.add)
        nc.sync.dma_start(out[0], res[:])
